import numpy as np
CORES = [4,132,260,388,12,140,268,396,20,148,276,404,28,156,284,412]
N = 16
ROWS, COLS = 4, 4
def setup_inputs(rng):
    return {"x": rng.standard_normal((N, 128, 256), dtype=np.float32)}
def reference(x):
    g = x.astype(np.float64).reshape(ROWS, COLS, 128, 256)
    rs = g.sum(axis=1)
    cs = g.sum(axis=0)
    y1 = np.stack([rs[r // COLS] for r in range(N)]).astype(x.dtype)
    y2 = np.stack([cs[r % COLS] for r in range(N)]).astype(x.dtype)
    return {"y1": y1, "y2": y2}

@@ -1,0 +1,100 @@
+from concourse.bass import DstId, RemoteDMATransfer
+from concourse.mybir import AluOpType
+
+COL = "W"
+HC = [2, 3, 6, 7]
+
+SCRATCH = {
+    "xs": ("dram", [8, 128, 32], "float32"),
+    "l1": ("dram", [8, 128, 32], "float32"),
+    "l2": ("dram", [8, 128, 32], "float32"),
+    "ce": ("dram", [8, 128, 32], "float32"),
+    "co": ("dram", [8, 128, 32], "float32"),
+    "h1": ("dram", [128, 32], "float32"),
+    "h2": ("dram", [128, 32], "float32"),
+    "h3": ("dram", [128, 32], "float32"),
+}
+SEMAPHORES = ["ld", "i1", "s1", "s2", "se", "so", "snt", "a1", "a2", "st"]
+
+
+def rank_program(g, core, T, topo):
+    h, k, lc = topo.host(core), topo.chip(core), core % 8
+    if k > 3 or (lc != 4 and lc not in HC):
+        return
+    S = T.sem
+    ADD = AluOpType.add
+
+    def cid(hh, kk, ll):
+        return hh * 128 + kk * 8 + ll
+
+    def did(dst):
+        rid, pid = topo.addr(dst, core)
+        return DstId(rid=rid, pnc=pid)
+
+    def xfer(srcs, dests, mask, sem):
+        return RemoteDMATransfer(dst_ids=[did(d) for d, _ in dests], dma_engine_mask=mask, remote_sem=sem,
+                                 srcs=srcs, dsts=[a for _, a in dests], alu_op=1 if len(srcs) > 1 else 0)
+
+    own = k >> 1
+    k2 = k ^ 2
+
+    if lc != 4:
+        j = HC.index(lc)
+        e = 4 * own + j
+        g.wait_ge(S.s1, 3)
+        if COL == "W":
+            g.remote_dma_fused([xfer([T.h1[:], T.h2[:]], [(cid(h, k ^ 1, lc), T.h3[:])], 0xFF, S.s2)], local_sem=S.snt)
+            g.wait_ge(S.s2, 8)
+            g.remote_dma_fused([xfer([T.h1[:], T.h2[:], T.h3[:]],
+                                     [(cid(h, k, 4), T.ce[e]), (cid(h, k2, 4), T.ce[e])], 0xFF, S.se)], local_sem=S.snt)
+            g.wait_ge(S.snt, 16)
+        else:
+            buf, sem = (T.ce, S.se) if k % 2 == 0 else (T.co, S.so)
+            g.remote_dma_fused([xfer([T.h1[:], T.h2[:]],
+                                     [(cid(h, kk, 4), buf[e]) for kk in (k, k2, k ^ 1, k ^ 3)], 0xFF, sem)], local_sem=S.snt)
+            g.wait_ge(S.snt, 8)
+        return
+
+    p, c = h ^ 1, 3 - h
+    g.sync.dma_start(T.xs[:], T.x[:]).then_inc(S.ld, 16)
+    g.sync.dma_start(T.y1[:], T.x[:]).then_inc(S.i1, 16)
+    g.wait_ge(S.ld, 16)
+    tr = []
+    for e in range(8):
+        if e // 4 == own:
+            tr.append(xfer([T.xs[e]], [(cid(p, k, 4), T.l1[e])], 1 << e, S.s1))
+        else:
+            tr.append(xfer([T.xs[e]], [(cid(h, k2, HC[e % 4]), T.h2[:]), (cid(c, k, 4), T.l1[e])], 1 << e, S.s1))
+    for j in range(4):
+        tr.append(xfer([T.xs[4 * own + j]], [(cid(h, k, HC[j]), T.h1[:])], 3 << (8 + 2 * j), S.s1))
+    g.remote_dma_fused(tr, local_sem=S.snt)
+
+    g.wait_ge(S.s1, 8)
+    tr = []
+    for e in range(8):
+        dst = cid(c, k, 4) if e // 4 == own else cid(p, k, 4)
+        tr.append(xfer([T.xs[e], T.l1[e]], [(dst, T.l2[e])], 1 << e, S.s2))
+    g.remote_dma_fused(tr, local_sem=S.snt)
+
+    g.wait_ge(S.i1, 16)
+    g.dma_start(T.y1[:], T.l1[:], accum_op=ADD, max_dma_last_dim=8192).then_inc(S.a1, 16)
+
+    if COL == "W":
+        g.sync.wait_ge(S.se, 64)
+        g.sync.dma_start(T.y2[:], T.ce[:]).then_inc(S.st, 16)
+    else:
+        A, sa, B, sb = (T.ce, S.se, T.co, S.so) if k % 2 == 0 else (T.co, S.so, T.ce, S.se)
+        g.sync.wait_ge(sa, 64)
+        g.sync.dma_start(T.y2[:], A[:]).then_inc(S.st, 16)
+
+    g.wait_ge(S.s2, 8)
+    g.wait_ge(S.a1, 16)
+    g.dma_start(T.y1[:], T.l2[:], accum_op=ADD, max_dma_last_dim=8192).then_inc(S.a1, 16)
+    if COL != "W":
+        g.wait_ge(sb, 64)
+        g.wait_ge(S.st, 16)
+        g.dma_start(T.y2[:], B[:], accum_op=ADD, max_dma_last_dim=8192).then_inc(S.a2, 16)
+        g.wait_ge(S.a2, 16)
+    g.wait_ge(S.a1, 32)
+    g.wait_ge(S.st, 16)
+    g.wait_ge(S.snt, 24)

@@ -1,28 +1,24 @@
 from concourse.bass import DstId, RemoteDMATransfer
-from concourse.mybir import AluOpType
 
-COL = "W"
-HC = [2, 3, 6, 7]
+ROWC, ROWS = [0, 1, 5, 5], [0, 0, 0, 1]
+COLC = [2, 3, 6, 7]
 
 SCRATCH = {
     "xs": ("dram", [8, 128, 32], "float32"),
-    "l1": ("dram", [8, 128, 32], "float32"),
-    "l2": ("dram", [8, 128, 32], "float32"),
-    "ce": ("dram", [8, 128, 32], "float32"),
-    "co": ("dram", [8, 128, 32], "float32"),
-    "h1": ("dram", [128, 32], "float32"),
-    "h2": ("dram", [128, 32], "float32"),
-    "h3": ("dram", [128, 32], "float32"),
+    "rs": ("dram", [8, 128, 32], "float32"),
+    "cs": ("dram", [8, 128, 32], "float32"),
+    "h1": ("dram", [2, 128, 32], "float32"),
+    "h2": ("dram", [2, 128, 32], "float32"),
+    "h3": ("dram", [2, 128, 32], "float32"),
 }
-SEMAPHORES = ["ld", "i1", "s1", "s2", "se", "so", "snt", "a1", "a2", "st"]
+SEMAPHORES = ["ld", "s1", "s2", "sr", "sc", "snt", "st"]
 
 
 def rank_program(g, core, T, topo):
     h, k, lc = topo.host(core), topo.chip(core), core % 8
-    if k > 3 or (lc != 4 and lc not in HC):
+    if k > 3:
         return
     S = T.sem
-    ADD = AluOpType.add
 
     def cid(hh, kk, ll):
         return hh * 128 + kk * 8 + ll
@@ -35,66 +31,49 @@ def rank_program(g, core, T, topo):
         return RemoteDMATransfer(dst_ids=[did(d) for d, _ in dests], dma_engine_mask=mask, remote_sem=sem,
                                  srcs=srcs, dsts=[a for _, a in dests], alu_op=1 if len(srcs) > 1 else 0)
 
-    own = k >> 1
-    k2 = k ^ 2
+    p, c, k2 = h ^ 1, 3 - h, k ^ 2
+    ro, co = (0 if h in (0, 3) else 1), k >> 1
 
     if lc != 4:
-        j = HC.index(lc)
-        e = 4 * own + j
-        g.wait_ge(S.s1, 3)
-        if COL == "W":
-            g.remote_dma_fused([xfer([T.h1[:], T.h2[:]], [(cid(h, k ^ 1, lc), T.h3[:])], 0xFF, S.s2)], local_sem=S.snt)
-            g.wait_ge(S.s2, 8)
-            g.remote_dma_fused([xfer([T.h1[:], T.h2[:], T.h3[:]],
-                                     [(cid(h, k, 4), T.ce[e]), (cid(h, k2, 4), T.ce[e])], 0xFF, S.se)], local_sem=S.snt)
-            g.wait_ge(S.snt, 16)
+        if lc in COLC:
+            js, half, slots = [COLC.index(lc)], co, [0]
+            peer, part, land, sem = cid(h, k ^ 1, lc), cid(h, k2, 4), T.cs, S.sc
         else:
-            buf, sem = (T.ce, S.se) if k % 2 == 0 else (T.co, S.so)
-            g.remote_dma_fused([xfer([T.h1[:], T.h2[:]],
-                                     [(cid(h, kk, 4), buf[e]) for kk in (k, k2, k ^ 1, k ^ 3)], 0xFF, sem)], local_sem=S.snt)
-            g.wait_ge(S.snt, 8)
+            js = [j for j in range(4) if ROWC[j] == lc]
+            half, slots = ro, [ROWS[j] for j in js]
+            peer, part, land, sem = cid(c, k, lc), cid(p, k, 4), T.rs, S.sr
+        n = 8 // len(js)
+        masks = [((1 << n) - 1) << (n * i) for i in range(len(js))]
+        g.wait_ge(S.s1, 3 * len(js))
+        g.remote_dma_fused([xfer([T.h1[s], T.h2[s]], [(peer, T.h3[s])], m, S.s2) for s, m in zip(slots, masks)],
+                           local_sem=S.snt)
+        g.wait_ge(S.s2, 8)
+        g.remote_dma_fused([xfer([T.h1[s], T.h2[s], T.h3[s]],
+                                 [(cid(h, k, 4), land[4 * half + j]), (part, land[4 * half + j])], m, sem)
+                            for j, s, m in zip(js, slots, masks)], local_sem=S.snt)
+        g.wait_ge(S.snt, 16)
         return
 
-    p, c = h ^ 1, 3 - h
     g.sync.dma_start(T.xs[:], T.x[:]).then_inc(S.ld, 16)
-    g.sync.dma_start(T.y1[:], T.x[:]).then_inc(S.i1, 16)
+    off, on = [], []
+    for e in range(8):
+        hf, j = e // 4, e % 4
+        o, i = [], []
+        (i if hf == ro else o).append((cid(h if hf == ro else p, k, ROWC[j]), (T.h1 if hf == ro else T.h2)[ROWS[j]]))
+        (i if hf == co else o).append((cid(h, k if hf == co else k2, COLC[j]), (T.h1 if hf == co else T.h2)[0]))
+        if o:
+            off.append((e, o))
+        if i:
+            on.append((e, i))
+    n = 8 // len(off)
+    tr = [xfer([T.xs[e]], d, ((1 << n) - 1) << (n * i), S.s1) for i, (e, d) in enumerate(off)]
+    tr += [xfer([T.xs[e]], d, ((1 << n) - 1) << (8 + n * i), S.s1) for i, (e, d) in enumerate(on)]
     g.wait_ge(S.ld, 16)
-    tr = []
-    for e in range(8):
-        if e // 4 == own:
-            tr.append(xfer([T.xs[e]], [(cid(p, k, 4), T.l1[e])], 1 << e, S.s1))
-        else:
-            tr.append(xfer([T.xs[e]], [(cid(h, k2, HC[e % 4]), T.h2[:]), (cid(c, k, 4), T.l1[e])], 1 << e, S.s1))
-    for j in range(4):
-        tr.append(xfer([T.xs[4 * own + j]], [(cid(h, k, HC[j]), T.h1[:])], 3 << (8 + 2 * j), S.s1))
     g.remote_dma_fused(tr, local_sem=S.snt)
 
-    g.wait_ge(S.s1, 8)
-    tr = []
-    for e in range(8):
-        dst = cid(c, k, 4) if e // 4 == own else cid(p, k, 4)
-        tr.append(xfer([T.xs[e], T.l1[e]], [(dst, T.l2[e])], 1 << e, S.s2))
-    g.remote_dma_fused(tr, local_sem=S.snt)
-
-    g.wait_ge(S.i1, 16)
-    g.dma_start(T.y1[:], T.l1[:], accum_op=ADD, max_dma_last_dim=8192).then_inc(S.a1, 16)
-
-    if COL == "W":
-        g.sync.wait_ge(S.se, 64)
-        g.sync.dma_start(T.y2[:], T.ce[:]).then_inc(S.st, 16)
-    else:
-        A, sa, B, sb = (T.ce, S.se, T.co, S.so) if k % 2 == 0 else (T.co, S.so, T.ce, S.se)
-        g.sync.wait_ge(sa, 64)
-        g.sync.dma_start(T.y2[:], A[:]).then_inc(S.st, 16)
-
-    g.wait_ge(S.s2, 8)
-    g.wait_ge(S.a1, 16)
-    g.dma_start(T.y1[:], T.l2[:], accum_op=ADD, max_dma_last_dim=8192).then_inc(S.a1, 16)
-    if COL != "W":
-        g.wait_ge(sb, 64)
-        g.wait_ge(S.st, 16)
-        g.dma_start(T.y2[:], B[:], accum_op=ADD, max_dma_last_dim=8192).then_inc(S.a2, 16)
-        g.wait_ge(S.a2, 16)
-    g.wait_ge(S.a1, 32)
-    g.wait_ge(S.st, 16)
-    g.wait_ge(S.snt, 24)
+    g.scalar.wait_ge(S.sr, 48)
+    g.scalar.dma_start(T.y1[:], T.rs[:]).then_inc(S.st, 16)
+    g.sync.wait_ge(S.sc, 64)
+    g.sync.dma_start(T.y2[:], T.cs[:]).then_inc(S.st, 16)
+    g.wait_ge(S.snt, 16)
+    g.wait_ge(S.st, 32)

@@ -1,6 +1,7 @@
 from concourse.bass import DstId, RemoteDMATransfer
 
-ROWC, ROWS = [0, 1, 5, 5], [0, 0, 0, 1]
+ROWC = [0, 5, 0, 5, 1, 5, 1, 5]
+ROWS = [0, 0, 0, 0, 0, 1, 0, 1]
 COLC = [2, 3, 6, 7]
 
 SCRATCH = {
@@ -31,43 +32,45 @@ def rank_program(g, core, T, topo):
         return RemoteDMATransfer(dst_ids=[did(d) for d, _ in dests], dma_engine_mask=mask, remote_sem=sem,
                                  srcs=srcs, dsts=[a for _, a in dests], alu_op=1 if len(srcs) > 1 else 0)
 
-    p, c, k2 = h ^ 1, 3 - h, k ^ 2
-    ro, co = (0 if h in (0, 3) else 1), k >> 1
+    p, c = h ^ 1, 3 - h
+
+    def row_owned(e):
+        return ((e % 4) // 2 == 0) == (h in ((0, 3) if e < 4 else (0, 1)))
+
+    def col_owned(e):
+        return e // 4 == k >> 1
+
+    tasks = [(ROWC[e], ROWS[e], e, (p, k) if e < 4 else (c, k), (c, k) if e < 4 else (p, k), T.rs, S.sr)
+             for e in range(8) if row_owned(e)]
+    tasks += [(COLC[e % 4], 0, e, (h, k ^ 2), (h, k ^ 1), T.cs, S.sc) for e in range(8) if col_owned(e)]
 
     if lc != 4:
-        if lc in COLC:
-            js, half, slots = [COLC.index(lc)], co, [0]
-            peer, part, land, sem = cid(h, k ^ 1, lc), cid(h, k2, 4), T.cs, S.sc
-        else:
-            js = [j for j in range(4) if ROWC[j] == lc]
-            half, slots = ro, [ROWS[j] for j in js]
-            peer, part, land, sem = cid(c, k, lc), cid(p, k, 4), T.rs, S.sr
-        n = 8 // len(js)
-        masks = [((1 << n) - 1) << (n * i) for i in range(len(js))]
-        g.wait_ge(S.s1, 3 * len(js))
-        g.remote_dma_fused([xfer([T.h1[s], T.h2[s]], [(peer, T.h3[s])], m, S.s2) for s, m in zip(slots, masks)],
-                           local_sem=S.snt)
+        mine = [t for t in tasks if t[0] == lc]
+        n = 8 // len(mine)
+        masks = [((1 << n) - 1) << (n * i) for i in range(len(mine))]
+        g.wait_ge(S.s1, 2 * len(mine))
+        g.remote_dma_fused([xfer([T.h1[s], T.h2[s]], [(cid(q2[0], q2[1], lc), T.h3[s])], m, S.s2)
+                            for (_, s, e, q1, q2, land, sem), m in zip(mine, masks)], local_sem=S.snt)
         g.wait_ge(S.s2, 8)
         g.remote_dma_fused([xfer([T.h1[s], T.h2[s], T.h3[s]],
-                                 [(cid(h, k, 4), land[4 * half + j]), (part, land[4 * half + j])], m, sem)
-                            for j, s, m in zip(js, slots, masks)], local_sem=S.snt)
+                                 [(cid(q1[0], q1[1], 4), land[e]), (cid(h, k, 4), land[e])], m, sem)
+                            for (_, s, e, q1, q2, land, sem), m in zip(mine, masks)], local_sem=S.snt)
         g.wait_ge(S.snt, 16)
         return
 
     g.sync.dma_start(T.xs[:], T.x[:]).then_inc(S.ld, 16)
     off, on = [], []
     for e in range(8):
-        hf, j = e // 4, e % 4
-        o, i = [], []
-        (i if hf == ro else o).append((cid(h if hf == ro else p, k, ROWC[j]), (T.h1 if hf == ro else T.h2)[ROWS[j]]))
-        (i if hf == co else o).append((cid(h, k if hf == co else k2, COLC[j]), (T.h1 if hf == co else T.h2)[0]))
-        if o:
-            off.append((e, o))
-        if i:
-            on.append((e, i))
-    n = 8 // len(off)
-    tr = [xfer([T.xs[e]], d, ((1 << n) - 1) << (n * i), S.s1) for i, (e, d) in enumerate(off)]
-    tr += [xfer([T.xs[e]], d, ((1 << n) - 1) << (8 + n * i), S.s1) for i, (e, d) in enumerate(on)]
+        if row_owned(e):
+            on.append((e, cid(h, k, ROWC[e]), T.h1[ROWS[e]]))
+        else:
+            off.append((e, cid(p if e < 4 else c, k, ROWC[e]), T.h2[ROWS[e]]))
+        if col_owned(e):
+            on.append((e, cid(h, k, COLC[e % 4]), T.h1[0]))
+        else:
+            off.append((e, cid(h, k ^ 2, COLC[e % 4]), T.h2[0]))
+    tr = [xfer([T.xs[e]], [(d, a)], 1 << i, S.s1) for i, (e, d, a) in enumerate(off)]
+    tr += [xfer([T.xs[e]], [(d, a)], 1 << (8 + i), S.s1) for i, (e, d, a) in enumerate(on)]
     g.wait_ge(S.ld, 16)
     g.remote_dma_fused(tr, local_sem=S.snt)
 

@@ -1,8 +1,9 @@
 from concourse.bass import DstId, RemoteDMATransfer
 
-ROWC = [0, 5, 0, 5, 1, 5, 1, 5]
-ROWS = [0, 0, 0, 0, 0, 1, 0, 1]
-COLC = [2, 3, 6, 7]
+NS = 6
+ROWC = [0, 2, 5, 0, 2, 5, 1, 1]
+COLC = [3, 3, 6, 3, 3, 6, 7, 7]
+COLS = [0, 1, 0, 0, 1, 0, 0, 0]
 
 SCRATCH = {
     "xs": ("dram", [8, 128, 32], "float32"),
@@ -34,49 +35,45 @@ def rank_program(g, core, T, topo):
 
     p, c = h ^ 1, 3 - h
 
-    def row_owned(e):
-        return ((e % 4) // 2 == 0) == (h in ((0, 3) if e < 4 else (0, 1)))
+    def owned(e):
+        base = ((e < 3) == (h in (0, 3))) if e < NS else ((e == 6) == (h in (0, 1)))
+        return base != (k >= 2)
 
-    def col_owned(e):
-        return e // 4 == k >> 1
-
-    tasks = [(ROWC[e], ROWS[e], e, (p, k) if e < 4 else (c, k), (c, k) if e < 4 else (p, k), T.rs, S.sr)
-             for e in range(8) if row_owned(e)]
-    tasks += [(COLC[e % 4], 0, e, (h, k ^ 2), (h, k ^ 1), T.cs, S.sc) for e in range(8) if col_owned(e)]
+    def q1h(e):
+        return p if e < NS else c
 
     if lc != 4:
-        mine = [t for t in tasks if t[0] == lc]
+        mine = [(0, e, (q1h(e), k), (c if e < NS else p, k), T.rs, S.sr) for e in range(8) if owned(e) and ROWC[e] == lc]
+        mine += [(COLS[e], e, (h, k ^ 2), (h, k ^ 1), T.cs, S.sc) for e in range(8) if owned(e) and COLC[e] == lc]
         n = 8 // len(mine)
         masks = [((1 << n) - 1) << (n * i) for i in range(len(mine))]
-        g.wait_ge(S.s1, 2 * len(mine))
+        g.wait_ge(S.s1, 4 * len(mine))
         g.remote_dma_fused([xfer([T.h1[s], T.h2[s]], [(cid(q2[0], q2[1], lc), T.h3[s])], m, S.s2)
-                            for (_, s, e, q1, q2, land, sem), m in zip(mine, masks)], local_sem=S.snt)
+                            for (s, e, q1, q2, land, sem), m in zip(mine, masks)], local_sem=S.snt)
         g.wait_ge(S.s2, 8)
         g.remote_dma_fused([xfer([T.h1[s], T.h2[s], T.h3[s]],
                                  [(cid(q1[0], q1[1], 4), land[e]), (cid(h, k, 4), land[e])], m, sem)
-                            for (_, s, e, q1, q2, land, sem), m in zip(mine, masks)], local_sem=S.snt)
+                            for (s, e, q1, q2, land, sem), m in zip(mine, masks)], local_sem=S.snt)
         g.wait_ge(S.snt, 16)
         return
 
     g.sync.dma_start(T.xs[:], T.x[:]).then_inc(S.ld, 16)
-    off, on = [], []
+    tr, noff, non = [], 0, 0
     for e in range(8):
-        if row_owned(e):
-            on.append((e, cid(h, k, ROWC[e]), T.h1[ROWS[e]]))
+        if owned(e):
+            tr.append(xfer([T.xs[e]], [(cid(h, k, ROWC[e]), T.h1[0]), (cid(h, k, COLC[e]), T.h1[COLS[e]])],
+                           3 << (8 + 2 * non), S.s1))
+            non += 1
         else:
-            off.append((e, cid(p if e < 4 else c, k, ROWC[e]), T.h2[ROWS[e]]))
-        if col_owned(e):
-            on.append((e, cid(h, k, COLC[e % 4]), T.h1[0]))
-        else:
-            off.append((e, cid(h, k ^ 2, COLC[e % 4]), T.h2[0]))
-    tr = [xfer([T.xs[e]], [(d, a)], 1 << i, S.s1) for i, (e, d, a) in enumerate(off)]
-    tr += [xfer([T.xs[e]], [(d, a)], 1 << (8 + i), S.s1) for i, (e, d, a) in enumerate(on)]
+            tr.append(xfer([T.xs[e]], [(cid(q1h(e), k, ROWC[e]), T.h2[0]), (cid(h, k ^ 2, COLC[e]), T.h2[COLS[e]])],
+                           3 << (2 * noff), S.s1))
+            noff += 1
     g.wait_ge(S.ld, 16)
     g.remote_dma_fused(tr, local_sem=S.snt)
 
-    g.scalar.wait_ge(S.sr, 48)
+    g.scalar.wait_ge(S.sr, 64)
     g.scalar.dma_start(T.y1[:], T.rs[:]).then_inc(S.st, 16)
-    g.sync.wait_ge(S.sc, 64)
+    g.sync.wait_ge(S.sc, 48)
     g.sync.dma_start(T.y2[:], T.cs[:]).then_inc(S.st, 16)
     g.wait_ge(S.snt, 16)
     g.wait_ge(S.st, 32)

from concourse.bass import DstId, RemoteDMATransfer

NS = 6
ROWC = [0, 2, 5, 0, 2, 5, 1, 1]
COLC = [3, 3, 6, 3, 3, 6, 7, 7]
COLS = [0, 1, 0, 0, 1, 0, 0, 0]

SCRATCH = {
    "xs": ("dram", [8, 128, 32], "float32"),
    "rs": ("dram", [8, 128, 32], "float32"),
    "cs": ("dram", [8, 128, 32], "float32"),
    "h1": ("dram", [2, 128, 32], "float32"),
    "h2": ("dram", [2, 128, 32], "float32"),
    "h3": ("dram", [2, 128, 32], "float32"),
}
SEMAPHORES = ["ld", "s1", "s2", "sr", "sc", "snt", "st"]


def rank_program(g, core, T, topo):
    h, k, lc = topo.host(core), topo.chip(core), core % 8
    if k > 3:
        return
    S = T.sem

    def cid(hh, kk, ll):
        return hh * 128 + kk * 8 + ll

    def did(dst):
        rid, pid = topo.addr(dst, core)
        return DstId(rid=rid, pnc=pid)

    def xfer(srcs, dests, mask, sem):
        return RemoteDMATransfer(dst_ids=[did(d) for d, _ in dests], dma_engine_mask=mask, remote_sem=sem,
                                 srcs=srcs, dsts=[a for _, a in dests], alu_op=1 if len(srcs) > 1 else 0)

    p, c = h ^ 1, 3 - h

    def owned(e):
        base = ((e < 3) == (h in (0, 3))) if e < NS else ((e == 6) == (h in (0, 1)))
        return base != (k >= 2)

    def q1h(e):
        return p if e < NS else c

    if lc != 4:
        mine = [(0, e, (q1h(e), k), (c if e < NS else p, k), T.rs, S.sr) for e in range(8) if owned(e) and ROWC[e] == lc]
        mine += [(COLS[e], e, (h, k ^ 2), (h, k ^ 1), T.cs, S.sc) for e in range(8) if owned(e) and COLC[e] == lc]
        n = 8 // len(mine)
        masks = [((1 << n) - 1) << (n * i) for i in range(len(mine))]
        g.wait_ge(S.s1, 4 * len(mine))
        g.remote_dma_fused([xfer([T.h1[s], T.h2[s]], [(cid(q2[0], q2[1], lc), T.h3[s])], m, S.s2)
                            for (s, e, q1, q2, land, sem), m in zip(mine, masks)], local_sem=S.snt)
        g.wait_ge(S.s2, 8)
        g.remote_dma_fused([xfer([T.h1[s], T.h2[s], T.h3[s]],
                                 [(cid(q1[0], q1[1], 4), land[e]), (cid(h, k, 4), land[e])], m, sem)
                            for (s, e, q1, q2, land, sem), m in zip(mine, masks)], local_sem=S.snt)
        g.wait_ge(S.snt, 16)
        return

    g.sync.dma_start(T.xs[:], T.x[:]).then_inc(S.ld, 16)
    tr, noff, non = [], 0, 0
    for e in range(8):
        if owned(e):
            tr.append(xfer([T.xs[e]], [(cid(h, k, ROWC[e]), T.h1[0]), (cid(h, k, COLC[e]), T.h1[COLS[e]])],
                           3 << (8 + 2 * non), S.s1))
            non += 1
        else:
            tr.append(xfer([T.xs[e]], [(cid(q1h(e), k, ROWC[e]), T.h2[0]), (cid(h, k ^ 2, COLC[e]), T.h2[COLS[e]])],
                           3 << (2 * noff), S.s1))
            noff += 1
    g.wait_ge(S.ld, 16)
    g.remote_dma_fused(tr, local_sem=S.snt)

    g.scalar.wait_ge(S.sr, 64)
    g.scalar.dma_start(T.y1[:], T.rs[:]).then_inc(S.st, 16)
    g.sync.wait_ge(S.sc, 48)
    g.sync.dma_start(T.y2[:], T.cs[:]).then_inc(S.st, 16)
    g.wait_ge(S.snt, 16)
    g.wait_ge(S.st, 32)
